import numpy as np, ml_dtypes
CORES = [10,11,138,139,266,267,394,395]
N = 8
def setup_inputs(rng):
    return {"x": rng.standard_normal((N, 128, 256), dtype=np.float32).astype(ml_dtypes.bfloat16)}
def reference(x):
    b = 256 // N
    blocks = x.reshape(N, 128, N, b)
    return {"y": np.ascontiguousarray(blocks.transpose(2, 1, 0, 3)).reshape(N, 128, 256)}

@@ -1,0 +1,81 @@
+from concourse.bass import DstId, RemoteDMATransfer
+
+SCRATCH = {
+    "xs": ("sbuf", [128, 256], "bfloat16"),
+    "land": ("sbuf", [128, 256], "bfloat16"),
+}
+SEMAPHORES = ["loaded", "arrived", "sent", "stored"]
+
+HOSTS = 4
+CABLE_HELPER, SWITCH_HELPER = 4, 6
+
+
+def _plan(T, topo):
+    cores = list(T.cores)
+    by_host = {}
+    for r, c in enumerate(cores):
+        by_host.setdefault(topo.host(c), []).append(r)
+    plan = []
+    for r, c in enumerate(cores):
+        h = topo.host(c)
+        step = 1 if by_host[h].index(r) == 0 else -1
+        via, far = (h + step) % HOSTS, (h + 2) % HOSTS
+        second_hop_is_cable = topo.rack(via) != topo.rack(far)
+        helper = via * 128 + topo.chip(c) * 8 + (CABLE_HELPER if second_hop_is_cable else SWITCH_HELPER)
+        plan.append((helper, by_host[far]))
+    return plan
+
+
+def rank_program(g, core, T, topo):
+    cores = list(T.cores)
+    n = len(cores)
+    b = T.xs.shape[1] // n
+    plan = _plan(T, topo)
+    rank = T.rank_of(core)
+
+    def blk(t, j, k=1):
+        return t[:, j * b:(j + k) * b]
+
+    def dst_id(d):
+        rid, pid = topo.addr(d, core)
+        return DstId(rid=rid, pnc=pid)
+
+    if rank is None:
+        srcs = [s for s in range(n) if plan[s][0] == core]
+        if not srcs:
+            return
+        s = srcs[0]
+        g.wait_ge(T.sem.arrived, 8)
+        g.remote_dma_fused(
+            [RemoteDMATransfer(dst_ids=[dst_id(cores[d])], dma_engine_mask=0x0F << (4 * i), remote_sem=T.sem.arrived,
+                               src=blk(T.xs, d), dst=blk(T.land, s))
+             for i, d in enumerate(plan[s][1])],
+            local_sem=T.sem.sent)
+        g.wait_ge(T.sem.sent, 8)
+        return
+
+    helper, far = plan[rank]
+    g.sync.dma_start(T.xs[:], T.x[:]).then_inc(T.sem.loaded, 16)
+    g.scalar.dma_start(blk(T.land, rank), blk(T.x, rank)).then_inc(T.sem.arrived, 16)
+    g.wait_ge(T.sem.loaded, 16)
+
+    rid, pid = topo.addr(helper, core)
+    g.remote_dma(blk(T.xs, far[0], len(far)), blk(T.xs, far[0], len(far)), T.sem.arrived, T.sem.sent, pid, rid, 0xFF)
+
+    transfers, off = [], 0
+    for d in range(n):
+        if d == rank or d in far:
+            continue
+        if topo.host(cores[d]) == topo.host(core):
+            m = 0xFF00
+        else:
+            m = 0x03 << (2 * off)
+            off += 1
+        transfers.append(RemoteDMATransfer(dst_ids=[dst_id(cores[d])], dma_engine_mask=m, remote_sem=T.sem.arrived,
+                                           src=blk(T.xs, d), dst=blk(T.land, rank)))
+    g.remote_dma_fused(transfers, local_sem=T.sem.sent)
+
+    g.wait_ge(T.sem.arrived, 16 + 8 + 4 * 2 + 2 * 4)
+    g.dma_start(T.y[:], T.land[:]).then_inc(T.sem.stored, 16)
+    g.wait_ge(T.sem.sent, 8 + 4 * 2 + 8)
+    g.wait_ge(T.sem.stored, 16)

@@ -75,7 +75,7 @@ def rank_program(g, core, T, topo):
                                            src=blk(T.xs, d), dst=blk(T.land, rank)))
     g.remote_dma_fused(transfers, local_sem=T.sem.sent)
 
-    g.wait_ge(T.sem.arrived, 16 + 8 + 4 * 2 + 2 * 4)
-    g.dma_start(T.y[:], T.land[:]).then_inc(T.sem.stored, 16)
+    g.sync.wait_ge(T.sem.arrived, 16 + 8 + 4 * 2 + 2 * 4)
+    g.sync.dma_start(T.y[:], T.land[:]).then_inc(T.sem.stored, 16)
     g.wait_ge(T.sem.sent, 8 + 4 * 2 + 8)
     g.wait_ge(T.sem.stored, 16)

from concourse.bass import DstId, RemoteDMATransfer

SCRATCH = {
    "xs": ("sbuf", [128, 256], "bfloat16"),
    "land": ("sbuf", [128, 256], "bfloat16"),
}
SEMAPHORES = ["loaded", "arrived", "sent", "stored"]

HOSTS = 4
CABLE_HELPER, SWITCH_HELPER = 4, 6


def _plan(T, topo):
    cores = list(T.cores)
    by_host = {}
    for r, c in enumerate(cores):
        by_host.setdefault(topo.host(c), []).append(r)
    plan = []
    for r, c in enumerate(cores):
        h = topo.host(c)
        step = 1 if by_host[h].index(r) == 0 else -1
        via, far = (h + step) % HOSTS, (h + 2) % HOSTS
        second_hop_is_cable = topo.rack(via) != topo.rack(far)
        helper = via * 128 + topo.chip(c) * 8 + (CABLE_HELPER if second_hop_is_cable else SWITCH_HELPER)
        plan.append((helper, by_host[far]))
    return plan


def rank_program(g, core, T, topo):
    cores = list(T.cores)
    n = len(cores)
    b = T.xs.shape[1] // n
    plan = _plan(T, topo)
    rank = T.rank_of(core)

    def blk(t, j, k=1):
        return t[:, j * b:(j + k) * b]

    def dst_id(d):
        rid, pid = topo.addr(d, core)
        return DstId(rid=rid, pnc=pid)

    if rank is None:
        srcs = [s for s in range(n) if plan[s][0] == core]
        if not srcs:
            return
        s = srcs[0]
        g.wait_ge(T.sem.arrived, 8)
        g.remote_dma_fused(
            [RemoteDMATransfer(dst_ids=[dst_id(cores[d])], dma_engine_mask=0x0F << (4 * i), remote_sem=T.sem.arrived,
                               src=blk(T.xs, d), dst=blk(T.land, s))
             for i, d in enumerate(plan[s][1])],
            local_sem=T.sem.sent)
        g.wait_ge(T.sem.sent, 8)
        return

    helper, far = plan[rank]
    g.sync.dma_start(T.xs[:], T.x[:]).then_inc(T.sem.loaded, 16)
    g.scalar.dma_start(blk(T.land, rank), blk(T.x, rank)).then_inc(T.sem.arrived, 16)
    g.wait_ge(T.sem.loaded, 16)

    rid, pid = topo.addr(helper, core)
    g.remote_dma(blk(T.xs, far[0], len(far)), blk(T.xs, far[0], len(far)), T.sem.arrived, T.sem.sent, pid, rid, 0xFF)

    transfers, off = [], 0
    for d in range(n):
        if d == rank or d in far:
            continue
        if topo.host(cores[d]) == topo.host(core):
            m = 0xFF00
        else:
            m = 0x03 << (2 * off)
            off += 1
        transfers.append(RemoteDMATransfer(dst_ids=[dst_id(cores[d])], dma_engine_mask=m, remote_sem=T.sem.arrived,
                                           src=blk(T.xs, d), dst=blk(T.land, rank)))
    g.remote_dma_fused(transfers, local_sem=T.sem.sent)

    g.sync.wait_ge(T.sem.arrived, 16 + 8 + 4 * 2 + 2 * 4)
    g.sync.dma_start(T.y[:], T.land[:]).then_inc(T.sem.stored, 16)
    g.wait_ge(T.sem.sent, 8 + 4 * 2 + 8)
    g.wait_ge(T.sem.stored, 16)
